import numpy as np
import ml_dtypes


def mxq(x, axis, fmt="e4m3"):
    dtype, down = {"e4m3": (ml_dtypes.float8_e4m3fn, 7), "e5m2": (ml_dtypes.float8_e5m2, 14)}[fmt]
    v = np.moveaxis(np.asarray(x, np.float32).astype(ml_dtypes.bfloat16).astype(np.float64), axis, -1)
    blocks = v.reshape(v.shape[:-1] + (-1, 32))
    amax = np.abs(blocks).max(-1, keepdims=True)
    byte = np.maximum(np.where(amax > 0, np.frexp(amax)[1] - 1 + 127, 0) - down, 1)
    scale = np.exp2(byte - 127.0)
    codes = (blocks / scale).astype(np.float32).astype(dtype).astype(np.float64)
    return np.moveaxis((codes * scale).reshape(v.shape), -1, axis)


WIDE = False


def mx_kscale(k):
    if not WIDE:
        return np.ones(k)
    levels = np.array([30, -30])
    if k % 512:
        return np.exp2(np.random.permutation(np.resize(levels, k // 32))).repeat(32)
    a = np.empty((k // 512, 16))
    for p in range(k // 512):
        a[p, :8] = np.random.permutation(np.resize(levels, 8))
        for g in range(8):
            far = levels[np.abs(levels - a[p, g]) >= 10]
            a[p, g + 8] = far[np.random.randint(len(far))]
    return np.exp2(a.ravel()).repeat(32)


BF16 = ml_dtypes.bfloat16


def bf(x):
    return np.asarray(x, np.float32).astype(BF16)


def f64(x):
    return np.asarray(x).astype(np.float64)


E2M1 = np.array([0.0, 0.5, 1.0, 1.5, 2.0, 3.0, 4.0, 6.0, -0.0, -0.5, -1.0, -1.5, -2.0, -3.0, -4.0, -6.0])


def pack_weight(w, fmt):
    k, n = w.shape
    w = f64(bf(w)).reshape(k // 32, 32, n)
    amax = np.abs(w).max(1)
    if fmt in ("e4m3", "e5m2"):
        byte = np.frexp(amax)[1] - 1 + 127 - (7 if fmt == "e4m3" else 14)
    else:
        mant, ex = np.frexp(amax / 6.0)
        byte = np.where(mant > 0.5, ex, ex - 1) + 127
    byte = np.clip(np.where(amax > 0, byte, 1), 1, 254)
    scaled = (w * np.exp2(127.0 - byte)[:, None, :]).reshape(k, n).astype(np.float32)
    by_word = np.ascontiguousarray(scaled.reshape(k // 512, 128, 4, n).transpose(0, 1, 3, 2))
    if fmt in ("e4m3", "e5m2"):
        words = by_word.astype(ml_dtypes.float8_e4m3fn if fmt == "e4m3" else ml_dtypes.float8_e5m2).view(np.uint8)
    else:
        c = by_word.astype(ml_dtypes.float4_e2m1fn).view(np.uint8) & 0xF
        words = c[..., 0::2] | (c[..., 1::2] << 4)
    return np.ascontiguousarray(words), np.ascontiguousarray(byte.astype(np.uint8).reshape(k // 512, 16, n))


def unpack_weight(words, scales, fmt):
    g, p, n, _ = words.shape
    if fmt in ("e4m3", "e5m2"):
        vals = np.ascontiguousarray(words).view(ml_dtypes.float8_e4m3fn if fmt == "e4m3" else ml_dtypes.float8_e5m2).astype(np.float64)
    else:
        nib = np.empty((g, p, n, 4), np.uint8)
        nib[..., 0::2] = words & 0xF
        nib[..., 1::2] = words >> 4
        vals = E2M1[nib]
    vals = vals * np.repeat(np.exp2(scales.astype(np.float64) - 127.0), 8, axis=1)[..., None]
    return vals.transpose(0, 1, 3, 2).reshape(g * 512, n)


P, K, F, J = 2048, 1024, 512, 1152


def setup_inputs():
    s, t = mx_kscale(K), mx_kscale(F)
    G = np.random.standard_normal((K, P)) * np.exp(0.5 * np.random.standard_normal((K, P))) * s[:, None]
    g_words, g_scales = pack_weight(G, "e5m2")
    return {"g_words": g_words,
            "g_scales": g_scales,
            "w": bf(np.random.standard_normal((K, J)) / np.sqrt(K) / s[:, None]),
            "e": bf(np.random.standard_normal((F, P)) * t[:, None]),
            "z": bf(np.random.standard_normal((F, P))),
            "v": bf(np.random.standard_normal((F, J)) / np.sqrt(F) / t[:, None]),
            "r": bf(0.5 + np.random.random_sample(P))}


def reference(g_words, g_scales, w, e, z, v, r):
    G = unpack_weight(g_words, g_scales, "e5m2")
    first = G.T @ mxq(f64(w), 0, "e4m3")
    b = f64(e) * (f64(z) > 0)
    second = mxq(b, 0, "e4m3").T @ mxq(f64(v), 0, "e4m3")
    return f64(r)[:, None] * (first + second)

@@ -1,0 +1,202 @@
+from contextlib import ExitStack
+
+import concourse.mybir as mybir
+
+POSITIONS, K, F, J = 2048, 1024, 512, 1152
+FLOPS = 2 * POSITIONS * (K + F) * J
+
+F32 = mybir.dt.float32
+BF16 = mybir.dt.bfloat16
+I32 = mybir.dt.int32
+U32 = mybir.dt.uint32
+U8 = mybir.dt.uint8
+E4M3 = mybir.dt.float8_e4m3fn_x4
+E5M2 = mybir.dt.float8_e5m2_x4
+ALU = mybir.AluOpType
+COPY = mybir.ActivationFunctionType.Copy
+
+P = 128
+PACK = 4
+K_PASS = P * PACK
+TILES = POSITIONS // P
+BANKS = 8
+BANK_COLS = 512
+COL_CHUNKS = [(0, 512), (512, 1024), (1024, 1152)]
+LOAD_SPANS = [(0, 512), (512, 1024), (1024, 2048)]
+SCALE_SPANS = [(0, 512), (512, 2048)]
+B_SPAN = 256
+RUN = 4
+OUT_BUFS = 10
+
+
+def span_of(spans, position):
+    for i, (lo, hi) in enumerate(spans):
+        if lo <= position < hi:
+            return i, position - lo
+    raise ValueError("position outside the spans")
+
+
+def tile_conv_patch_gradient_e4_kernel(tc, g_words, g_scales, w, e, z, v, r, out):
+    nc = tc.nc
+    with ExitStack() as ctx:
+        keep = ctx.enter_context(tc.tile_pool(name="keep", bufs=1))
+        stage = ctx.enter_context(tc.tile_pool(name="stage", bufs=2))
+        outs = ctx.enter_context(tc.tile_pool(name="outs", bufs=OUT_BUFS))
+        psum = ctx.enter_context(tc.psum_pool(name="psum", bufs=1))
+        ctx.enter_context(tc.manual_schedule())
+
+        def load_rows(name, rows, lo, hi):
+            raw = keep.tile([P, PACK, hi - lo], BF16, name=name, align_bytes=64)
+            nc.sync.dma_start(out=raw[:], in_=rows.rearrange("(p t) n -> p t n", t=PACK)[:, :, lo:hi])
+            return raw
+
+        def load_g_words(i):
+            lo, hi = LOAD_SPANS[i]
+            words = keep.tile([P, K // K_PASS, hi - lo], U32, name="g_words%d" % i, align_bytes=64)
+            src = g_words.rearrange("g p n t -> p g (n t)")[:, :, PACK * lo : PACK * hi]
+            nc.sync.dma_start(out=words[:].bitcast(I32), in_=src.bitcast(I32))
+            return words
+
+        def load_g_scales(i, queue):
+            lo, hi = SCALE_SPANS[i]
+            plane = keep.tile([P, K // K_PASS, hi - lo], U8, name="g_scales%d" % i, align_bytes=64)
+            for q in range(4):
+                src = g_scales[:, 4 * q : 4 * q + 4, lo:hi].rearrange("g r n -> r g n")
+                queue.dma_start(out=plane[32 * q : 32 * q + 4, :, :].bitcast(I32), in_=src.bitcast(I32))
+            return plane
+
+        r_rows = keep.tile([P, 64], BF16, name="r_rows", align_bytes=64)
+        nc.scalar.dma_start(out=r_rows[0:32, :], in_=r.rearrange("(q c) -> q c", c=64))
+        g_planes = [load_g_scales(0, nc.scalar)]
+
+        e_raw = [load_rows("e0", e, *LOAD_SPANS[0])]
+        z_raw = [load_rows("z0", z, *LOAD_SPANS[0])]
+        filters = [load_rows("v", v, 0, J), load_rows("w0", w[0:K_PASS, :], 0, J)]
+        g_tiles = [load_g_words(0)]
+        filters.append(load_rows("w1", w[K_PASS:K, :], 0, J))
+        for i in range(1, len(LOAD_SPANS)):
+            e_raw.append(load_rows("e%d" % i, e, *LOAD_SPANS[i]))
+            z_raw.append(load_rows("z%d" % i, z, *LOAD_SPANS[i]))
+            g_tiles.append(load_g_words(i))
+            if i < len(SCALE_SPANS):
+                g_planes.append(load_g_scales(i, nc.sync))
+
+        r_words = r_rows[:].bitcast(I32)
+        for a in range(1, 4):
+            half = 16 * (a % 2)
+            nc.vector.tensor_copy(out=r_words[32 * a : 32 * a + 32, 0:16], in_=r_words[0:32, half : half + 16])
+        r_turned = keep.tile([P, 32], BF16, name="r_turned", align_bytes=64)
+        nc.vector.transpose(r_turned[:], r_rows[:, 0:32])
+        r_cols = keep.tile([P, TILES], F32, name="r_cols")
+        for h in range(2):
+            rows = slice(64 * h, 64 * h + 64)
+            nc.scalar.activation(out=r_cols[rows, :], in_=r_turned[rows, h:32:2], func=COPY)
+
+        def interleave(copy, raw, pool, name, tag):
+            width = raw.shape[2]
+            grouped = pool.tile([P, width, PACK], BF16, name=name, tag=tag, align_bytes=64)
+            copy(
+                out=grouped[:].rearrange("p (c i) t -> p c t i", i=RUN),
+                in_=raw.rearrange("p t (c i) -> p c t i", i=RUN),
+            )
+            return grouped
+
+        def quantise(grouped, name):
+            width = grouped.shape[1]
+            codes = keep.tile([P, width], U32, name=name + "_codes", align_bytes=64)
+            plane = keep.tile([P, width], U8, name=name + "_scales", align_bytes=64)
+            nc.vector.quantize_mx(
+                out=codes[:].bitcast(E4M3), scales=plane[:], in_=grouped[:].rearrange("p n t -> p (n t)")
+            )
+            return codes, plane
+
+        b_quant = {}
+
+        def make_b(pair, second_copy):
+            spans = (2 * pair, 2 * pair + 1)
+            gates, products, grouped = {}, {}, {}
+            for s in spans:
+                i, lo = span_of(LOAD_SPANS, s * B_SPAN)
+                gates[s] = stage.tile([P, PACK, B_SPAN], BF16, name="mask", align_bytes=64)
+                nc.vector.tensor_scalar(
+                    out=gates[s][:], in0=z_raw[i][:, :, lo : lo + B_SPAN], scalar1=0.0, scalar2=None, op0=ALU.is_gt
+                )
+            for s in spans:
+                i, lo = span_of(LOAD_SPANS, s * B_SPAN)
+                products[s] = stage.tile([P, PACK, B_SPAN], BF16, name="product", align_bytes=64)
+                nc.vector.tensor_tensor(
+                    out=products[s][:], in0=e_raw[i][:, :, lo : lo + B_SPAN], in1=gates[s][:], op=ALU.mult
+                )
+            for s, copy in zip(spans, (nc.vector.tensor_copy, second_copy)):
+                grouped[s] = interleave(copy, products[s][:], stage, "b_grouped", "b_grouped")
+            for s in spans:
+                b_quant[s] = quantise(grouped[s], "b%d" % s)
+
+        filter_quant = {}
+
+        def make_filter(f):
+            grouped = []
+            for c, (lo, hi) in enumerate(COL_CHUNKS):
+                copy = nc.vector.tensor_copy if c == 0 else nc.scalar.copy
+                name = "filter%d_%d" % (f, c)
+                grouped.append(interleave(copy, filters[f][:, :, lo:hi], keep, name, name))
+            for c in range(len(COL_CHUNKS)):
+                filter_quant[(f, c)] = quantise(grouped[c], "filter%d_%d" % (f, c))
+
+        def multiply(acc, m, c, f, start, stop):
+            if f == 0:
+                codes, plane = b_quant[m * P // B_SPAN]
+                lo = m * P % B_SPAN
+                lhs, lhs_scale = codes[:, lo : lo + P].bitcast(E4M3), plane[:, lo : lo + P]
+            else:
+                i, lo = span_of(LOAD_SPANS, m * P)
+                lhs = g_tiles[i][:, f - 1, lo : lo + P].bitcast(E5M2)
+                i, lo = span_of(SCALE_SPANS, m * P)
+                lhs_scale = g_planes[i][:, f - 1, lo : lo + P]
+            codes, plane = filter_quant[(f, c)]
+            nc.tensor.matmul_mx(
+                out=acc, lhsT=lhs, lhsT_scale=lhs_scale, rhs=codes[:].bitcast(E4M3), rhs_scale=plane[:],
+                start=start, stop=stop,
+            )
+
+        groups = [(m, c) for m in range(TILES) for c in range(len(COL_CHUNKS))]
+        head = sorted(groups[:BANKS], key=lambda mc: (mc[1], mc[0]))
+        results = {}
+
+        def open_bank(n, c):
+            lo, hi = COL_CHUNKS[c]
+            bank = psum.tile([P, BANK_COLS], F32, name="bank%d" % (n % BANKS))
+            return bank[:, 0 : hi - lo]
+
+        def finish(acc, m, c):
+            lo, hi = COL_CHUNKS[c]
+            if m not in results:
+                results[m] = outs.tile([P, J], F32, name="result")
+            last = m == TILES - 1
+            if last and c == 1:
+                nc.vector.tensor_scalar(
+                    out=results[m][:, lo:hi], in0=acc, scalar1=r_cols[:, m : m + 1], scalar2=None, op0=ALU.mult
+                )
+            else:
+                nc.scalar.activation(out=results[m][:, lo:hi], in_=acc, func=COPY, scale=r_cols[:, m : m + 1])
+            rows = slice(m * P, (m + 1) * P)
+            if last:
+                nc.sync.dma_start(out=out[rows, lo:hi], in_=results[m][:, lo:hi])
+            elif c == len(COL_CHUNKS) - 1:
+                nc.sync.dma_start(out=out[rows, :], in_=results[m][:])
+
+        make_b(0, nc.scalar.copy)
+        head_accs = [open_bank(n, c) for n, (m, c) in enumerate(head)]
+        for f in range(3):
+            make_filter(f)
+            for acc, (m, c) in zip(head_accs, head):
+                multiply(acc, m, c, f, f == 0, f == 2)
+        for acc, (m, c) in zip(head_accs, head):
+            finish(acc, m, c)
+        for n, (m, c) in enumerate(groups[BANKS:]):
+            if m * P // B_SPAN not in b_quant:
+                make_b(m * P // (2 * B_SPAN), nc.vector.tensor_copy)
+            acc = open_bank(n, c)
+            for f in (1, 2, 0):
+                multiply(acc, m, c, f, f == 1, f == 0)
+            finish(acc, m, c)

@@ -22,11 +22,12 @@ TILES = POSITIONS // P
 BANKS = 8
 BANK_COLS = 512
 COL_CHUNKS = [(0, 512), (512, 1024), (1024, 1152)]
-LOAD_SPANS = [(0, 512), (512, 1024), (1024, 2048)]
-SCALE_SPANS = [(0, 512), (512, 2048)]
+EZ_SPANS = [(0, 512), (512, 1024), (1024, 2048)]
+G_SPANS = [(1536, 2048), (0, 512), (512, 1536)]
+EARLY_TILES = 4
 B_SPAN = 256
 RUN = 4
-OUT_BUFS = 10
+OUT_BUFS = 8
 
 
 def span_of(spans, position):
@@ -51,35 +52,35 @@ def tile_conv_patch_gradient_e4_kernel(tc, g_words, g_scales, w, e, z, v, r, out
             return raw
 
         def load_g_words(i):
-            lo, hi = LOAD_SPANS[i]
+            lo, hi = G_SPANS[i]
             words = keep.tile([P, K // K_PASS, hi - lo], U32, name="g_words%d" % i, align_bytes=64)
             src = g_words.rearrange("g p n t -> p g (n t)")[:, :, PACK * lo : PACK * hi]
             nc.sync.dma_start(out=words[:].bitcast(I32), in_=src.bitcast(I32))
             return words
 
-        def load_g_scales(i, queue):
-            lo, hi = SCALE_SPANS[i]
-            plane = keep.tile([P, K // K_PASS, hi - lo], U8, name="g_scales%d" % i, align_bytes=64)
-            for q in range(4):
-                src = g_scales[:, 4 * q : 4 * q + 4, lo:hi].rearrange("g r n -> r g n")
-                queue.dma_start(out=plane[32 * q : 32 * q + 4, :, :].bitcast(I32), in_=src.bitcast(I32))
+        def load_g_scales():
+            plane = keep.tile([P, K // K_PASS, POSITIONS], U8, name="g_plane", align_bytes=64)
+            for row in range(4):
+                src = g_scales.rearrange("g (q s) n -> s q g n", s=4)[row]
+                nc.sync.dma_start(out=plane[row:P:32, :, :].bitcast(I32), in_=src.bitcast(I32))
             return plane
 
         r_rows = keep.tile([P, 64], BF16, name="r_rows", align_bytes=64)
         nc.scalar.dma_start(out=r_rows[0:32, :], in_=r.rearrange("(q c) -> q c", c=64))
-        g_planes = [load_g_scales(0, nc.scalar)]
 
-        e_raw = [load_rows("e0", e, *LOAD_SPANS[0])]
-        z_raw = [load_rows("z0", z, *LOAD_SPANS[0])]
-        filters = [load_rows("v", v, 0, J), load_rows("w0", w[0:K_PASS, :], 0, J)]
+        filters = {1: load_rows("w0", w[0:K_PASS, :], 0, J)}
+        g_plane = load_g_scales()
         g_tiles = [load_g_words(0)]
-        filters.append(load_rows("w1", w[K_PASS:K, :], 0, J))
-        for i in range(1, len(LOAD_SPANS)):
-            e_raw.append(load_rows("e%d" % i, e, *LOAD_SPANS[i]))
-            z_raw.append(load_rows("z%d" % i, z, *LOAD_SPANS[i]))
-            g_tiles.append(load_g_words(i))
-            if i < len(SCALE_SPANS):
-                g_planes.append(load_g_scales(i, nc.sync))
+        filters[2] = load_rows("w1", w[K_PASS:K, :], 0, J)
+        g_tiles.append(load_g_words(1))
+        e_raw = [load_rows("e0", e, *EZ_SPANS[0])]
+        z_raw = [load_rows("z0", z, *EZ_SPANS[0])]
+        filters[0] = load_rows("v", v, 0, J)
+        e_raw.append(load_rows("e1", e, *EZ_SPANS[1]))
+        z_raw.append(load_rows("z1", z, *EZ_SPANS[1]))
+        g_tiles.append(load_g_words(2))
+        e_raw.append(load_rows("e2", e, *EZ_SPANS[2]))
+        z_raw.append(load_rows("z2", z, *EZ_SPANS[2]))
 
         r_words = r_rows[:].bitcast(I32)
         for a in range(1, 4):
@@ -112,36 +113,47 @@ def tile_conv_patch_gradient_e4_kernel(tc, g_words, g_scales, w, e, z, v, r, out
 
         b_quant = {}
 
-        def make_b(pair, second_copy):
-            spans = (2 * pair, 2 * pair + 1)
+        def make_b(spans):
             gates, products, grouped = {}, {}, {}
             for s in spans:
-                i, lo = span_of(LOAD_SPANS, s * B_SPAN)
+                i, lo = span_of(EZ_SPANS, s * B_SPAN)
                 gates[s] = stage.tile([P, PACK, B_SPAN], BF16, name="mask", align_bytes=64)
                 nc.vector.tensor_scalar(
                     out=gates[s][:], in0=z_raw[i][:, :, lo : lo + B_SPAN], scalar1=0.0, scalar2=None, op0=ALU.is_gt
                 )
             for s in spans:
-                i, lo = span_of(LOAD_SPANS, s * B_SPAN)
+                i, lo = span_of(EZ_SPANS, s * B_SPAN)
                 products[s] = stage.tile([P, PACK, B_SPAN], BF16, name="product", align_bytes=64)
                 nc.vector.tensor_tensor(
                     out=products[s][:], in0=e_raw[i][:, :, lo : lo + B_SPAN], in1=gates[s][:], op=ALU.mult
                 )
-            for s, copy in zip(spans, (nc.vector.tensor_copy, second_copy)):
-                grouped[s] = interleave(copy, products[s][:], stage, "b_grouped", "b_grouped")
+            for s in spans:
+                grouped[s] = interleave(nc.vector.tensor_copy, products[s][:], stage, "b_grouped", "b_grouped")
             for s in spans:
                 b_quant[s] = quantise(grouped[s], "b%d" % s)
 
         filter_quant = {}
 
-        def make_filter(f):
-            grouped = []
-            for c, (lo, hi) in enumerate(COL_CHUNKS):
-                copy = nc.vector.tensor_copy if c == 0 else nc.scalar.copy
-                name = "filter%d_%d" % (f, c)
-                grouped.append(interleave(copy, filters[f][:, :, lo:hi], keep, name, name))
-            for c in range(len(COL_CHUNKS)):
-                filter_quant[(f, c)] = quantise(grouped[c], "filter%d_%d" % (f, c))
+        def group_filter(f, c, copy):
+            lo, hi = COL_CHUNKS[c]
+            name = "filter%d_%d" % (f, c)
+            return interleave(copy, filters[f][:, :, lo:hi], keep, name, name)
+
+        def quantise_filter(f, c, grouped):
+            filter_quant[(f, c)] = quantise(grouped, "filter%d_%d" % (f, c))
+
+        def make_w(f):
+            grouped = [group_filter(f, c, nc.vector.tensor_copy if c == 0 else nc.scalar.copy) for c in range(3)]
+            for c in range(3):
+                quantise_filter(f, c, grouped[c])
+
+        def make_v():
+            wide0 = group_filter(0, 0, nc.vector.tensor_copy)
+            narrow = group_filter(0, 2, nc.vector.tensor_copy)
+            quantise_filter(0, 0, wide0)
+            wide1 = group_filter(0, 1, nc.vector.tensor_copy)
+            quantise_filter(0, 2, narrow)
+            quantise_filter(0, 1, wide1)
 
         def multiply(acc, m, c, f, start, stop):
             if f == 0:
@@ -149,54 +161,100 @@ def tile_conv_patch_gradient_e4_kernel(tc, g_words, g_scales, w, e, z, v, r, out
                 lo = m * P % B_SPAN
                 lhs, lhs_scale = codes[:, lo : lo + P].bitcast(E4M3), plane[:, lo : lo + P]
             else:
-                i, lo = span_of(LOAD_SPANS, m * P)
+                i, lo = span_of(G_SPANS, m * P)
                 lhs = g_tiles[i][:, f - 1, lo : lo + P].bitcast(E5M2)
-                i, lo = span_of(SCALE_SPANS, m * P)
-                lhs_scale = g_planes[i][:, f - 1, lo : lo + P]
+                lhs_scale = g_plane[:, f - 1, m * P : (m + 1) * P]
             codes, plane = filter_quant[(f, c)]
             nc.tensor.matmul_mx(
                 out=acc, lhsT=lhs, lhsT_scale=lhs_scale, rhs=codes[:].bitcast(E4M3), rhs_scale=plane[:],
                 start=start, stop=stop,
             )
 
-        groups = [(m, c) for m in range(TILES) for c in range(len(COL_CHUNKS))]
-        head = sorted(groups[:BANKS], key=lambda mc: (mc[1], mc[0]))
-        results = {}
+        free_banks = list(range(BANKS))
+        accs, results, done = {}, {}, {}
 
-        def open_bank(n, c):
+        def open_group(m, c):
             lo, hi = COL_CHUNKS[c]
-            bank = psum.tile([P, BANK_COLS], F32, name="bank%d" % (n % BANKS))
-            return bank[:, 0 : hi - lo]
+            n = free_banks[0]
+            free_banks.remove(n)
+            bank = psum.tile([P, BANK_COLS], F32, name="bank%d" % n)
+            accs[(m, c)] = (n, bank[:, 0 : hi - lo])
 
-        def finish(acc, m, c):
+        def passes(m, c, fs, first, last):
+            for f in fs:
+                multiply(accs[(m, c)][1], m, c, f, f == first, f == last)
+
+        def scale_out(m, c):
             lo, hi = COL_CHUNKS[c]
+            n, acc = accs[(m, c)]
+            nc.scalar.activation(out=results[m][:, lo:hi], in_=acc, func=COPY, scale=r_cols[:, m : m + 1])
+            free_banks.append(n)
+
+        def add_out(m, c):
+            lo, hi = COL_CHUNKS[c]
+            n, acc = accs[(m, c)]
+            part = results[m][:, lo:hi]
+            nc.vector.scalar_tensor_tensor(
+                out=part, in0=acc, scalar=r_cols[:, m : m + 1], in1=part, op0=ALU.mult, op1=ALU.add
+            )
+            free_banks.append(n)
+
+        def store(m, c):
+            done[m] = done.get(m, 0) + 1
+            if m == TILES - EARLY_TILES - 1:
+                lo, hi = COL_CHUNKS[c]
+                nc.sync.dma_start(out=out[m * P : (m + 1) * P, lo:hi], in_=results[m][:, lo:hi])
+            elif done[m] == len(COL_CHUNKS):
+                nc.sync.dma_start(out=out[m * P : (m + 1) * P, :], in_=results[m][:])
+
+        def finish(m, c):
             if m not in results:
                 results[m] = outs.tile([P, J], F32, name="result")
-            last = m == TILES - 1
-            if last and c == 1:
-                nc.vector.tensor_scalar(
-                    out=results[m][:, lo:hi], in0=acc, scalar1=r_cols[:, m : m + 1], scalar2=None, op0=ALU.mult
-                )
-            else:
-                nc.scalar.activation(out=results[m][:, lo:hi], in_=acc, func=COPY, scale=r_cols[:, m : m + 1])
-            rows = slice(m * P, (m + 1) * P)
-            if last:
-                nc.sync.dma_start(out=out[rows, lo:hi], in_=results[m][:, lo:hi])
-            elif c == len(COL_CHUNKS) - 1:
-                nc.sync.dma_start(out=out[rows, :], in_=results[m][:])
+            scale_out(m, c)
+            store(m, c)
 
-        make_b(0, nc.scalar.copy)
-        head_accs = [open_bank(n, c) for n, (m, c) in enumerate(head)]
-        for f in range(3):
-            make_filter(f)
-            for acc, (m, c) in zip(head_accs, head):
-                multiply(acc, m, c, f, f == 0, f == 2)
-        for acc, (m, c) in zip(head_accs, head):
-            finish(acc, m, c)
-        for n, (m, c) in enumerate(groups[BANKS:]):
-            if m * P // B_SPAN not in b_quant:
-                make_b(m * P // (2 * B_SPAN), nc.vector.tensor_copy)
-            acc = open_bank(n, c)
-            for f in (1, 2, 0):
-                multiply(acc, m, c, f, f == 1, f == 0)
-            finish(acc, m, c)
+        def groups_of(tiles):
+            return [(m, c) for m in tiles for c in range(len(COL_CHUNKS))]
+
+        early_tiles = list(range(TILES - EARLY_TILES, TILES))
+        plain_tiles = list(range(TILES - EARLY_TILES))
+        early, plain = groups_of(early_tiles), groups_of(plain_tiles)
+        for m in early_tiles:
+            results[m] = keep.tile([P, J], F32, name="early%d" % m)
+
+        first = sorted(early[:BANKS], key=lambda mc: (mc[1], mc[0]))
+        for f in (1, 2):
+            make_w(f)
+            for m, c in first:
+                if f == 1:
+                    open_group(m, c)
+                passes(m, c, (f,), 1, 2)
+        for m, c in first:
+            scale_out(m, c)
+        for m, c in early[BANKS:]:
+            open_group(m, c)
+            passes(m, c, (1, 2), 1, 2)
+            scale_out(m, c)
+
+        for m, c in plain[:BANKS]:
+            open_group(m, c)
+            passes(m, c, (1, 2), 1, 0)
+        make_b((0, 1))
+        make_v()
+        for m, c in sorted(plain[:BANKS], key=lambda mc: ((0, 2, 1)[mc[1]], mc[0])):
+            passes(m, c, (0,), 1, 0)
+            finish(m, c)
+
+        for spans in ((2, 3), (6, 4), (7, 5)):
+            make_b(spans)
+        for m, c in plain[BANKS:]:
+            partner = m + EARLY_TILES
+            if partner in early_tiles and c == 0:
+                for c2 in range(len(COL_CHUNKS)):
+                    open_group(partner, c2)
+                    passes(partner, c2, (0,), 0, 0)
+                    add_out(partner, c2)
+                    store(partner, c2)
+            open_group(m, c)
+            passes(m, c, (1, 2, 0), 1, 0)
+            finish(m, c)

@@ -27,7 +27,6 @@ G_SPANS = [(1536, 2048), (0, 512), (512, 1536)]
 EARLY_TILES = 4
 B_SPAN = 256
 RUN = 4
-OUT_BUFS = 8
 
 
 def span_of(spans, position):
@@ -42,24 +41,23 @@ def tile_conv_patch_gradient_e4_kernel(tc, g_words, g_scales, w, e, z, v, r, out
     with ExitStack() as ctx:
         keep = ctx.enter_context(tc.tile_pool(name="keep", bufs=1))
         stage = ctx.enter_context(tc.tile_pool(name="stage", bufs=2))
-        outs = ctx.enter_context(tc.tile_pool(name="outs", bufs=OUT_BUFS))
         psum = ctx.enter_context(tc.psum_pool(name="psum", bufs=1))
         ctx.enter_context(tc.manual_schedule())
 
         def load_rows(name, rows, lo, hi):
-            raw = keep.tile([P, PACK, hi - lo], BF16, name=name, align_bytes=64)
+            raw = keep.tile([P, PACK, hi - lo], BF16, name=name, align_bytes=256)
             nc.sync.dma_start(out=raw[:], in_=rows.rearrange("(p t) n -> p t n", t=PACK)[:, :, lo:hi])
             return raw
 
         def load_g_words(i):
             lo, hi = G_SPANS[i]
-            words = keep.tile([P, K // K_PASS, hi - lo], U32, name="g_words%d" % i, align_bytes=64)
+            words = keep.tile([P, K // K_PASS, hi - lo], U32, name="g_words%d" % i, align_bytes=256)
             src = g_words.rearrange("g p n t -> p g (n t)")[:, :, PACK * lo : PACK * hi]
             nc.sync.dma_start(out=words[:].bitcast(I32), in_=src.bitcast(I32))
             return words
 
         def load_g_scales():
-            plane = keep.tile([P, K // K_PASS, POSITIONS], U8, name="g_plane", align_bytes=64)
+            plane = keep.tile([P, K // K_PASS, POSITIONS], U8, name="g_plane", align_bytes=256)
             for row in range(4):
                 src = g_scales.rearrange("g (q s) n -> s q g n", s=4)[row]
                 nc.sync.dma_start(out=plane[row:P:32, :, :].bitcast(I32), in_=src.bitcast(I32))
@@ -199,17 +197,22 @@ def tile_conv_patch_gradient_e4_kernel(tc, g_words, g_scales, w, e, z, v, r, out
             )
             free_banks.append(n)
 
+        last_tile = TILES - EARLY_TILES - 1
+
         def store(m, c):
-            done[m] = done.get(m, 0) + 1
-            if m == TILES - EARLY_TILES - 1:
-                lo, hi = COL_CHUNKS[c]
+            pair = m // 2
+            done[pair] = done.get(pair, 0) + 1
+            lo, hi = COL_CHUNKS[c]
+            if m == last_tile:
                 nc.sync.dma_start(out=out[m * P : (m + 1) * P, lo:hi], in_=results[m][:, lo:hi])
-            elif done[m] == len(COL_CHUNKS):
-                nc.sync.dma_start(out=out[m * P : (m + 1) * P, :], in_=results[m][:])
+            elif m == last_tile - 1:
+                if c == len(COL_CHUNKS) - 1:
+                    nc.sync.dma_start(out=out[m * P : (m + 1) * P, :], in_=results[m])
+            elif done[pair] == 2 * len(COL_CHUNKS):
+                rows = out[2 * pair * P : 2 * (pair + 1) * P, :].rearrange("(a p) j -> p a j", p=P)
+                nc.sync.dma_start(out=rows, in_=pair_results[pair][:])
 
         def finish(m, c):
-            if m not in results:
-                results[m] = outs.tile([P, J], F32, name="result")
             scale_out(m, c)
             store(m, c)
 
@@ -219,8 +222,9 @@ def tile_conv_patch_gradient_e4_kernel(tc, g_words, g_scales, w, e, z, v, r, out
         early_tiles = list(range(TILES - EARLY_TILES, TILES))
         plain_tiles = list(range(TILES - EARLY_TILES))
         early, plain = groups_of(early_tiles), groups_of(plain_tiles)
-        for m in early_tiles:
-            results[m] = keep.tile([P, J], F32, name="early%d" % m)
+        pair_results = [keep.tile([P, 2, J], F32, name="result%d" % i, align_bytes=256) for i in range(TILES // 2)]
+        for m in range(TILES):
+            results[m] = pair_results[m // 2][:, m % 2, :]
 
         first = sorted(early[:BANKS], key=lambda mc: (mc[1], mc[0]))
         for f in (1, 2):

@@ -16,24 +16,33 @@ ALU = mybir.AluOpType
 COPY = mybir.ActivationFunctionType.Copy
 
 P = 128
+QUAD = 32
 PACK = 4
 K_PASS = P * PACK
+G_PASSES = K // K_PASS
 TILES = POSITIONS // P
 BANKS = 8
 BANK_COLS = 512
-COL_CHUNKS = [(0, 512), (512, 1024), (1024, 1152)]
-EZ_SPANS = [(0, 512), (512, 1024), (1024, 2048)]
-G_SPANS = [(1536, 2048), (0, 512), (512, 1536)]
+
+CHUNKS = [(0, 512), (512, 1024), (1024, J)]
+FIRST, SECOND, NARROW = 0, 1, 2
+
+W0, W1, V = "w0", "w1", "v"
+
 EARLY_TILES = 4
+PLAIN_TILES = TILES - EARLY_TILES
+
+G_SPANS = [(1536, 2048), (0, 512), (512, 1536)]
+EZ_SPANS = [(0, 512), (512, 1024), (1024, 2048)]
 B_SPAN = 256
+
 RUN = 4
+Z1_AFTER = 5
 
 
 def span_of(spans, position):
-    for i, (lo, hi) in enumerate(spans):
-        if lo <= position < hi:
-            return i, position - lo
-    raise ValueError("position outside the spans")
+    i = [lo <= position < hi for lo, hi in spans].index(True)
+    return i, position - spans[i][0]
 
 
 def tile_conv_patch_gradient_e4_kernel(tc, g_words, g_scales, w, e, z, v, r, out):
@@ -44,56 +53,72 @@ def tile_conv_patch_gradient_e4_kernel(tc, g_words, g_scales, w, e, z, v, r, out
         psum = ctx.enter_context(tc.psum_pool(name="psum", bufs=1))
         ctx.enter_context(tc.manual_schedule())
 
-        def load_rows(name, rows, lo, hi):
+        filter_rows, e_rows, z_rows, g_codes, g_planes = {}, {}, {}, {}, {}
+
+        def load_rows(queue, name, rows, lo, hi):
             raw = keep.tile([P, PACK, hi - lo], BF16, name=name, align_bytes=256)
-            nc.sync.dma_start(out=raw[:], in_=rows.rearrange("(p t) n -> p t n", t=PACK)[:, :, lo:hi])
+            queue.dma_start(out=raw[:], in_=rows.rearrange("(p t) n -> p t n", t=PACK)[:, :, lo:hi])
             return raw
 
-        def load_g_words(i):
+        def load_filter(name, rows):
+            filter_rows[name] = load_rows(nc.sync, name, rows, 0, J)
+
+        def load_e(i):
+            e_rows[i] = load_rows(nc.sync, "e%d" % i, e, *EZ_SPANS[i])
+
+        def load_z(i, queue):
+            z_rows[i] = load_rows(queue, "z%d" % i, z, *EZ_SPANS[i])
+
+        def g_codes_tile(i):
             lo, hi = G_SPANS[i]
-            words = keep.tile([P, K // K_PASS, hi - lo], U32, name="g_words%d" % i, align_bytes=256)
-            src = g_words.rearrange("g p n t -> p g (n t)")[:, :, PACK * lo : PACK * hi]
-            nc.sync.dma_start(out=words[:].bitcast(I32), in_=src.bitcast(I32))
-            return words
+            g_codes[i] = keep.tile([P, G_PASSES, hi - lo], U32, name="g_codes%d" % i, align_bytes=256)
 
-        def load_g_scales():
-            plane = keep.tile([P, K // K_PASS, POSITIONS], U8, name="g_plane", align_bytes=256)
-            for row in range(4):
-                src = g_scales.rearrange("g (q s) n -> s q g n", s=4)[row]
-                nc.sync.dma_start(out=plane[row:P:32, :, :].bitcast(I32), in_=src.bitcast(I32))
-            return plane
+        def load_g_codes(i, queue, passes):
+            lo, hi = G_SPANS[i]
+            src = g_words.rearrange("g p n t -> p g (n t)")[:, passes, PACK * lo : PACK * hi]
+            queue.dma_start(out=g_codes[i][:, passes, :].bitcast(I32), in_=src.bitcast(I32))
 
-        r_rows = keep.tile([P, 64], BF16, name="r_rows", align_bytes=64)
-        nc.scalar.dma_start(out=r_rows[0:32, :], in_=r.rearrange("(q c) -> q c", c=64))
+        def load_g_scales(i):
+            lo, hi = G_SPANS[i]
+            plane = keep.tile([P, G_PASSES, hi - lo], U8, name="g_plane%d" % i, align_bytes=256)
+            for s in range(4):
+                src = g_scales.rearrange("g (q s) n -> s q g n", s=4)[s][:, :, lo:hi]
+                nc.sync.dma_start(out=plane[s:P:QUAD, :, :].bitcast(I32), in_=src.bitcast(I32))
+            g_planes[i] = plane
 
-        filters = {1: load_rows("w0", w[0:K_PASS, :], 0, J)}
-        g_plane = load_g_scales()
-        g_tiles = [load_g_words(0)]
-        filters[2] = load_rows("w1", w[K_PASS:K, :], 0, J)
-        g_tiles.append(load_g_words(1))
-        e_raw = [load_rows("e0", e, *EZ_SPANS[0])]
-        z_raw = [load_rows("z0", z, *EZ_SPANS[0])]
-        filters[0] = load_rows("v", v, 0, J)
-        e_raw.append(load_rows("e1", e, *EZ_SPANS[1]))
-        z_raw.append(load_rows("z1", z, *EZ_SPANS[1]))
-        g_tiles.append(load_g_words(2))
-        e_raw.append(load_rows("e2", e, *EZ_SPANS[2]))
-        z_raw.append(load_rows("z2", z, *EZ_SPANS[2]))
+        both_passes = slice(0, G_PASSES)
+        for i in range(len(G_SPANS)):
+            g_codes_tile(i)
+
+        r_rows = keep.tile([P, 2 * QUAD], BF16, name="r_rows", align_bytes=64)
+        nc.scalar.dma_start(out=r_rows[0:QUAD, :], in_=r.rearrange("(q c) -> q c", c=2 * QUAD))
+
+        load_filter(W0, w[0:K_PASS, :])
+        load_g_scales(0)
+        load_g_codes(0, nc.sync, slice(0, 1))
+        load_filter(W1, w[K_PASS:K, :])
+        load_g_codes(0, nc.sync, slice(1, 2))
+        load_g_scales(1)
+        load_z(0, nc.sync)
+        load_e(0)
+        load_filter(V, v)
 
         r_words = r_rows[:].bitcast(I32)
-        for a in range(1, 4):
-            half = 16 * (a % 2)
-            nc.vector.tensor_copy(out=r_words[32 * a : 32 * a + 32, 0:16], in_=r_words[0:32, half : half + 16])
-        r_turned = keep.tile([P, 32], BF16, name="r_turned", align_bytes=64)
-        nc.vector.transpose(r_turned[:], r_rows[:, 0:32])
+        half_words = QUAD // 2
+        for a in range(1, P // QUAD):
+            lo = half_words * (a % 2)
+            nc.vector.tensor_copy(
+                out=r_words[QUAD * a : QUAD * (a + 1), 0:half_words], in_=r_words[0:QUAD, lo : lo + half_words]
+            )
+        r_turned = keep.tile([P, QUAD], BF16, name="r_turned", align_bytes=64)
+        nc.vector.transpose(r_turned[:], r_rows[:, 0:QUAD])
         r_cols = keep.tile([P, TILES], F32, name="r_cols")
         for h in range(2):
-            rows = slice(64 * h, 64 * h + 64)
-            nc.scalar.activation(out=r_cols[rows, :], in_=r_turned[rows, h:32:2], func=COPY)
+            rows = slice(2 * QUAD * h, 2 * QUAD * (h + 1))
+            nc.scalar.activation(out=r_cols[rows, :], in_=r_turned[rows, h:QUAD:2], func=COPY)
 
-        def interleave(copy, raw, pool, name, tag):
-            width = raw.shape[2]
-            grouped = pool.tile([P, width, PACK], BF16, name=name, tag=tag, align_bytes=64)
+        def interleave(copy, raw, pool, name):
+            grouped = pool.tile([P, raw.shape[2], PACK], BF16, name=name, align_bytes=64)
             copy(
                 out=grouped[:].rearrange("p (c i) t -> p c t i", i=RUN),
                 in_=raw.rearrange("p t (c i) -> p c t i", i=RUN),
@@ -103,162 +128,166 @@ def tile_conv_patch_gradient_e4_kernel(tc, g_words, g_scales, w, e, z, v, r, out
         def quantise(grouped, name):
             width = grouped.shape[1]
             codes = keep.tile([P, width], U32, name=name + "_codes", align_bytes=64)
-            plane = keep.tile([P, width], U8, name=name + "_scales", align_bytes=64)
+            plane = keep.tile([P, width], U8, name=name + "_plane", align_bytes=64)
             nc.vector.quantize_mx(
                 out=codes[:].bitcast(E4M3), scales=plane[:], in_=grouped[:].rearrange("p n t -> p (n t)")
             )
             return codes, plane
 
-        b_quant = {}
+        filter_mx, b_mx = {}, {}
 
-        def make_b(spans):
+        def interleave_filter(name, c, copy):
+            lo, hi = CHUNKS[c]
+            return interleave(copy, filter_rows[name][:, :, lo:hi], keep, "%s_grouped%d" % (name, c))
+
+        def quantise_filter(name, c, grouped):
+            filter_mx[(name, c)] = quantise(grouped, "%s_%d" % (name, c))
+
+        def make_b(pieces):
             gates, products, grouped = {}, {}, {}
-            for s in spans:
-                i, lo = span_of(EZ_SPANS, s * B_SPAN)
-                gates[s] = stage.tile([P, PACK, B_SPAN], BF16, name="mask", align_bytes=64)
+            for piece in pieces:
+                i, lo = span_of(EZ_SPANS, piece * B_SPAN)
+                gates[piece] = stage.tile([P, PACK, B_SPAN], BF16, name="gate", align_bytes=64)
                 nc.vector.tensor_scalar(
-                    out=gates[s][:], in0=z_raw[i][:, :, lo : lo + B_SPAN], scalar1=0.0, scalar2=None, op0=ALU.is_gt
+                    out=gates[piece][:], in0=z_rows[i][:, :, lo : lo + B_SPAN], scalar1=0.0, scalar2=None, op0=ALU.is_gt
                 )
-            for s in spans:
-                i, lo = span_of(EZ_SPANS, s * B_SPAN)
-                products[s] = stage.tile([P, PACK, B_SPAN], BF16, name="product", align_bytes=64)
+            for piece in pieces:
+                i, lo = span_of(EZ_SPANS, piece * B_SPAN)
+                products[piece] = stage.tile([P, PACK, B_SPAN], BF16, name="product", align_bytes=64)
                 nc.vector.tensor_tensor(
-                    out=products[s][:], in0=e_raw[i][:, :, lo : lo + B_SPAN], in1=gates[s][:], op=ALU.mult
+                    out=products[piece][:], in0=e_rows[i][:, :, lo : lo + B_SPAN], in1=gates[piece][:], op=ALU.mult
                 )
-            for s in spans:
-                grouped[s] = interleave(nc.vector.tensor_copy, products[s][:], stage, "b_grouped", "b_grouped")
-            for s in spans:
-                b_quant[s] = quantise(grouped[s], "b%d" % s)
+            for piece in pieces:
+                grouped[piece] = interleave(nc.vector.tensor_copy, products[piece][:], stage, "b_grouped")
+            for piece in pieces:
+                b_mx[piece] = quantise(grouped[piece], "b%d" % piece)
 
-        filter_quant = {}
+        results = [keep.tile([P, J], F32, name="result%d" % m, align_bytes=256) for m in range(TILES)]
+        free_banks = list(range(BANKS))
+        accs, chunks_done, stores = {}, {}, []
 
-        def group_filter(f, c, copy):
-            lo, hi = COL_CHUNKS[c]
-            name = "filter%d_%d" % (f, c)
-            return interleave(copy, filters[f][:, :, lo:hi], keep, name, name)
+        def open_group(m, c):
+            lo, hi = CHUNKS[c]
+            bank = free_banks[0]
+            free_banks.remove(bank)
+            whole_bank = psum.tile([P, BANK_COLS], F32, name="bank%d" % bank)
+            accs[(m, c)] = (bank, whole_bank[:, 0 : hi - lo])
 
-        def quantise_filter(f, c, grouped):
-            filter_quant[(f, c)] = quantise(grouped, "filter%d_%d" % (f, c))
-
-        def make_w(f):
-            grouped = [group_filter(f, c, nc.vector.tensor_copy if c == 0 else nc.scalar.copy) for c in range(3)]
-            for c in range(3):
-                quantise_filter(f, c, grouped[c])
-
-        def make_v():
-            wide0 = group_filter(0, 0, nc.vector.tensor_copy)
-            narrow = group_filter(0, 2, nc.vector.tensor_copy)
-            quantise_filter(0, 0, wide0)
-            wide1 = group_filter(0, 1, nc.vector.tensor_copy)
-            quantise_filter(0, 2, narrow)
-            quantise_filter(0, 1, wide1)
-
-        def multiply(acc, m, c, f, start, stop):
-            if f == 0:
-                codes, plane = b_quant[m * P // B_SPAN]
+        def multiply(m, c, name, start, stop):
+            if name == V:
+                codes, plane = b_mx[m * P // B_SPAN]
                 lo = m * P % B_SPAN
                 lhs, lhs_scale = codes[:, lo : lo + P].bitcast(E4M3), plane[:, lo : lo + P]
             else:
+                g = (W0, W1).index(name)
                 i, lo = span_of(G_SPANS, m * P)
-                lhs = g_tiles[i][:, f - 1, lo : lo + P].bitcast(E5M2)
-                lhs_scale = g_plane[:, f - 1, m * P : (m + 1) * P]
-            codes, plane = filter_quant[(f, c)]
+                lhs, lhs_scale = g_codes[i][:, g, lo : lo + P].bitcast(E5M2), g_planes[i][:, g, lo : lo + P]
+            codes, plane = filter_mx[(name, c)]
             nc.tensor.matmul_mx(
-                out=acc, lhsT=lhs, lhsT_scale=lhs_scale, rhs=codes[:].bitcast(E4M3), rhs_scale=plane[:],
-                start=start, stop=stop,
+                out=accs[(m, c)][1],
+                lhsT=lhs,
+                lhsT_scale=lhs_scale,
+                rhs=codes[:].bitcast(E4M3),
+                rhs_scale=plane[:],
+                start=start,
+                stop=stop,
             )
 
-        free_banks = list(range(BANKS))
-        accs, results, done = {}, {}, {}
-
-        def open_group(m, c):
-            lo, hi = COL_CHUNKS[c]
-            n = free_banks[0]
-            free_banks.remove(n)
-            bank = psum.tile([P, BANK_COLS], F32, name="bank%d" % n)
-            accs[(m, c)] = (n, bank[:, 0 : hi - lo])
-
-        def passes(m, c, fs, first, last):
-            for f in fs:
-                multiply(accs[(m, c)][1], m, c, f, f == first, f == last)
-
         def scale_out(m, c):
-            lo, hi = COL_CHUNKS[c]
-            n, acc = accs[(m, c)]
+            lo, hi = CHUNKS[c]
+            bank, acc = accs[(m, c)]
             nc.scalar.activation(out=results[m][:, lo:hi], in_=acc, func=COPY, scale=r_cols[:, m : m + 1])
-            free_banks.append(n)
+            free_banks.append(bank)
 
         def add_out(m, c):
-            lo, hi = COL_CHUNKS[c]
-            n, acc = accs[(m, c)]
+            lo, hi = CHUNKS[c]
+            bank, acc = accs[(m, c)]
             part = results[m][:, lo:hi]
             nc.vector.scalar_tensor_tensor(
                 out=part, in0=acc, scalar=r_cols[:, m : m + 1], in1=part, op0=ALU.mult, op1=ALU.add
             )
-            free_banks.append(n)
+            free_banks.append(bank)
 
-        last_tile = TILES - EARLY_TILES - 1
+        def store(m, lo, hi):
+            queue = (nc.sync, nc.scalar)[len(stores) % 2]
+            stores.append(m)
+            queue.dma_start(out=out[m * P : (m + 1) * P, lo:hi], in_=results[m][:, lo:hi])
 
-        def store(m, c):
-            pair = m // 2
-            done[pair] = done.get(pair, 0) + 1
-            lo, hi = COL_CHUNKS[c]
-            if m == last_tile:
-                nc.sync.dma_start(out=out[m * P : (m + 1) * P, lo:hi], in_=results[m][:, lo:hi])
-            elif m == last_tile - 1:
-                if c == len(COL_CHUNKS) - 1:
-                    nc.sync.dma_start(out=out[m * P : (m + 1) * P, :], in_=results[m])
-            elif done[pair] == 2 * len(COL_CHUNKS):
-                rows = out[2 * pair * P : 2 * (pair + 1) * P, :].rearrange("(a p) j -> p a j", p=P)
-                nc.sync.dma_start(out=rows, in_=pair_results[pair][:])
+        def chunk_done(m, c):
+            chunks_done[m] = chunks_done.get(m, 0) + 1
+            whole = chunks_done[m] == len(CHUNKS)
+            if m == PLAIN_TILES - 1:
+                if c == FIRST:
+                    store(m, *CHUNKS[FIRST])
+                elif whole:
+                    store(m, CHUNKS[SECOND][0], J)
+            elif whole:
+                store(m, 0, J)
 
-        def finish(m, c):
-            scale_out(m, c)
-            store(m, c)
+        early = [(m, c) for m in range(PLAIN_TILES, TILES) for c in range(len(CHUNKS))]
+        plain = [(m, c) for m in range(PLAIN_TILES) for c in range(len(CHUNKS))]
 
-        def groups_of(tiles):
-            return [(m, c) for m in tiles for c in range(len(COL_CHUNKS))]
-
-        early_tiles = list(range(TILES - EARLY_TILES, TILES))
-        plain_tiles = list(range(TILES - EARLY_TILES))
-        early, plain = groups_of(early_tiles), groups_of(plain_tiles)
-        pair_results = [keep.tile([P, 2, J], F32, name="result%d" % i, align_bytes=256) for i in range(TILES // 2)]
-        for m in range(TILES):
-            results[m] = pair_results[m // 2][:, m % 2, :]
-
-        first = sorted(early[:BANKS], key=lambda mc: (mc[1], mc[0]))
-        for f in (1, 2):
-            make_w(f)
-            for m, c in first:
-                if f == 1:
+        opening = sorted(early[:BANKS], key=lambda group: (group[1], group[0]))
+        for name in (W0, W1):
+            grouped = {FIRST: interleave_filter(name, FIRST, nc.vector.tensor_copy)}
+            grouped[SECOND] = interleave_filter(name, SECOND, nc.scalar.copy)
+            if name == W1:
+                load_g_codes(1, nc.scalar, both_passes)
+                load_e(1)
+            grouped[NARROW] = interleave_filter(name, NARROW, nc.scalar.copy)
+            for c in range(len(CHUNKS)):
+                quantise_filter(name, c, grouped[c])
+            for m, c in opening:
+                if name == W0:
                     open_group(m, c)
-                passes(m, c, (f,), 1, 2)
-        for m, c in first:
+                multiply(m, c, name, start=name == W0, stop=name == W1)
+        for n, (m, c) in enumerate(opening):
+            if n == Z1_AFTER:
+                load_z(1, nc.scalar)
+                load_g_codes(2, nc.sync, both_passes)
+                load_g_scales(2)
             scale_out(m, c)
         for m, c in early[BANKS:]:
             open_group(m, c)
-            passes(m, c, (1, 2), 1, 2)
+            multiply(m, c, W0, start=True, stop=False)
+            multiply(m, c, W1, start=False, stop=True)
             scale_out(m, c)
+        load_z(2, nc.scalar)
+        load_e(2)
 
         for m, c in plain[:BANKS]:
             open_group(m, c)
-            passes(m, c, (1, 2), 1, 0)
+            multiply(m, c, W0, start=True, stop=False)
+            multiply(m, c, W1, start=False, stop=False)
         make_b((0, 1))
-        make_v()
-        for m, c in sorted(plain[:BANKS], key=lambda mc: ((0, 2, 1)[mc[1]], mc[0])):
-            passes(m, c, (0,), 1, 0)
-            finish(m, c)
+        v_order = (FIRST, NARROW, SECOND)
+        grouped = {}
+        for n, c in enumerate(v_order):
+            grouped[c] = interleave_filter(V, c, nc.vector.tensor_copy)
+            if n > 0:
+                quantise_filter(V, v_order[n - 1], grouped[v_order[n - 1]])
+        quantise_filter(V, v_order[-1], grouped[v_order[-1]])
+        for m, c in sorted(plain[:BANKS], key=lambda group: (v_order.index(group[1]), group[0])):
+            multiply(m, c, V, start=False, stop=True)
+            scale_out(m, c)
+            chunk_done(m, c)
 
-        for spans in ((2, 3), (6, 4), (7, 5)):
-            make_b(spans)
+        make_b((2, 3))
+        partner_step = EARLY_TILES * P // B_SPAN
+        for piece in range((PLAIN_TILES - EARLY_TILES) * P // B_SPAN, PLAIN_TILES * P // B_SPAN):
+            make_b((piece + partner_step, piece))
+
         for m, c in plain[BANKS:]:
             partner = m + EARLY_TILES
-            if partner in early_tiles and c == 0:
-                for c2 in range(len(COL_CHUNKS)):
-                    open_group(partner, c2)
-                    passes(partner, c2, (0,), 0, 0)
-                    add_out(partner, c2)
-                    store(partner, c2)
+            if c == FIRST and partner >= PLAIN_TILES:
+                for partner_c in range(len(CHUNKS)):
+                    open_group(partner, partner_c)
+                    multiply(partner, partner_c, V, start=True, stop=True)
+                    add_out(partner, partner_c)
+                    chunk_done(partner, partner_c)
             open_group(m, c)
-            passes(m, c, (1, 2, 0), 1, 0)
-            finish(m, c)
+            multiply(m, c, W0, start=True, stop=False)
+            multiply(m, c, W1, start=False, stop=False)
+            multiply(m, c, V, start=False, stop=True)
+            scale_out(m, c)
+            chunk_done(m, c)

from contextlib import ExitStack

import concourse.mybir as mybir

POSITIONS, K, F, J = 2048, 1024, 512, 1152
FLOPS = 2 * POSITIONS * (K + F) * J

F32 = mybir.dt.float32
BF16 = mybir.dt.bfloat16
I32 = mybir.dt.int32
U32 = mybir.dt.uint32
U8 = mybir.dt.uint8
E4M3 = mybir.dt.float8_e4m3fn_x4
E5M2 = mybir.dt.float8_e5m2_x4
ALU = mybir.AluOpType
COPY = mybir.ActivationFunctionType.Copy

P = 128
QUAD = 32
PACK = 4
K_PASS = P * PACK
G_PASSES = K // K_PASS
TILES = POSITIONS // P
BANKS = 8
BANK_COLS = 512

CHUNKS = [(0, 512), (512, 1024), (1024, J)]
FIRST, SECOND, NARROW = 0, 1, 2

W0, W1, V = "w0", "w1", "v"

EARLY_TILES = 4
PLAIN_TILES = TILES - EARLY_TILES

G_SPANS = [(1536, 2048), (0, 512), (512, 1536)]
EZ_SPANS = [(0, 512), (512, 1024), (1024, 2048)]
B_SPAN = 256

RUN = 4
Z1_AFTER = 5


def span_of(spans, position):
    i = [lo <= position < hi for lo, hi in spans].index(True)
    return i, position - spans[i][0]


def tile_conv_patch_gradient_e4_kernel(tc, g_words, g_scales, w, e, z, v, r, out):
    nc = tc.nc
    with ExitStack() as ctx:
        keep = ctx.enter_context(tc.tile_pool(name="keep", bufs=1))
        stage = ctx.enter_context(tc.tile_pool(name="stage", bufs=2))
        psum = ctx.enter_context(tc.psum_pool(name="psum", bufs=1))
        ctx.enter_context(tc.manual_schedule())

        filter_rows, e_rows, z_rows, g_codes, g_planes = {}, {}, {}, {}, {}

        def load_rows(queue, name, rows, lo, hi):
            raw = keep.tile([P, PACK, hi - lo], BF16, name=name, align_bytes=256)
            queue.dma_start(out=raw[:], in_=rows.rearrange("(p t) n -> p t n", t=PACK)[:, :, lo:hi])
            return raw

        def load_filter(name, rows):
            filter_rows[name] = load_rows(nc.sync, name, rows, 0, J)

        def load_e(i):
            e_rows[i] = load_rows(nc.sync, "e%d" % i, e, *EZ_SPANS[i])

        def load_z(i, queue):
            z_rows[i] = load_rows(queue, "z%d" % i, z, *EZ_SPANS[i])

        def g_codes_tile(i):
            lo, hi = G_SPANS[i]
            g_codes[i] = keep.tile([P, G_PASSES, hi - lo], U32, name="g_codes%d" % i, align_bytes=256)

        def load_g_codes(i, queue, passes):
            lo, hi = G_SPANS[i]
            src = g_words.rearrange("g p n t -> p g (n t)")[:, passes, PACK * lo : PACK * hi]
            queue.dma_start(out=g_codes[i][:, passes, :].bitcast(I32), in_=src.bitcast(I32))

        def load_g_scales(i):
            lo, hi = G_SPANS[i]
            plane = keep.tile([P, G_PASSES, hi - lo], U8, name="g_plane%d" % i, align_bytes=256)
            for s in range(4):
                src = g_scales.rearrange("g (q s) n -> s q g n", s=4)[s][:, :, lo:hi]
                nc.sync.dma_start(out=plane[s:P:QUAD, :, :].bitcast(I32), in_=src.bitcast(I32))
            g_planes[i] = plane

        both_passes = slice(0, G_PASSES)
        for i in range(len(G_SPANS)):
            g_codes_tile(i)

        r_rows = keep.tile([P, 2 * QUAD], BF16, name="r_rows", align_bytes=64)
        nc.scalar.dma_start(out=r_rows[0:QUAD, :], in_=r.rearrange("(q c) -> q c", c=2 * QUAD))

        load_filter(W0, w[0:K_PASS, :])
        load_g_scales(0)
        load_g_codes(0, nc.sync, slice(0, 1))
        load_filter(W1, w[K_PASS:K, :])
        load_g_codes(0, nc.sync, slice(1, 2))
        load_g_scales(1)
        load_z(0, nc.sync)
        load_e(0)
        load_filter(V, v)

        r_words = r_rows[:].bitcast(I32)
        half_words = QUAD // 2
        for a in range(1, P // QUAD):
            lo = half_words * (a % 2)
            nc.vector.tensor_copy(
                out=r_words[QUAD * a : QUAD * (a + 1), 0:half_words], in_=r_words[0:QUAD, lo : lo + half_words]
            )
        r_turned = keep.tile([P, QUAD], BF16, name="r_turned", align_bytes=64)
        nc.vector.transpose(r_turned[:], r_rows[:, 0:QUAD])
        r_cols = keep.tile([P, TILES], F32, name="r_cols")
        for h in range(2):
            rows = slice(2 * QUAD * h, 2 * QUAD * (h + 1))
            nc.scalar.activation(out=r_cols[rows, :], in_=r_turned[rows, h:QUAD:2], func=COPY)

        def interleave(copy, raw, pool, name):
            grouped = pool.tile([P, raw.shape[2], PACK], BF16, name=name, align_bytes=64)
            copy(
                out=grouped[:].rearrange("p (c i) t -> p c t i", i=RUN),
                in_=raw.rearrange("p t (c i) -> p c t i", i=RUN),
            )
            return grouped

        def quantise(grouped, name):
            width = grouped.shape[1]
            codes = keep.tile([P, width], U32, name=name + "_codes", align_bytes=64)
            plane = keep.tile([P, width], U8, name=name + "_plane", align_bytes=64)
            nc.vector.quantize_mx(
                out=codes[:].bitcast(E4M3), scales=plane[:], in_=grouped[:].rearrange("p n t -> p (n t)")
            )
            return codes, plane

        filter_mx, b_mx = {}, {}

        def interleave_filter(name, c, copy):
            lo, hi = CHUNKS[c]
            return interleave(copy, filter_rows[name][:, :, lo:hi], keep, "%s_grouped%d" % (name, c))

        def quantise_filter(name, c, grouped):
            filter_mx[(name, c)] = quantise(grouped, "%s_%d" % (name, c))

        def make_b(pieces):
            gates, products, grouped = {}, {}, {}
            for piece in pieces:
                i, lo = span_of(EZ_SPANS, piece * B_SPAN)
                gates[piece] = stage.tile([P, PACK, B_SPAN], BF16, name="gate", align_bytes=64)
                nc.vector.tensor_scalar(
                    out=gates[piece][:], in0=z_rows[i][:, :, lo : lo + B_SPAN], scalar1=0.0, scalar2=None, op0=ALU.is_gt
                )
            for piece in pieces:
                i, lo = span_of(EZ_SPANS, piece * B_SPAN)
                products[piece] = stage.tile([P, PACK, B_SPAN], BF16, name="product", align_bytes=64)
                nc.vector.tensor_tensor(
                    out=products[piece][:], in0=e_rows[i][:, :, lo : lo + B_SPAN], in1=gates[piece][:], op=ALU.mult
                )
            for piece in pieces:
                grouped[piece] = interleave(nc.vector.tensor_copy, products[piece][:], stage, "b_grouped")
            for piece in pieces:
                b_mx[piece] = quantise(grouped[piece], "b%d" % piece)

        results = [keep.tile([P, J], F32, name="result%d" % m, align_bytes=256) for m in range(TILES)]
        free_banks = list(range(BANKS))
        accs, chunks_done, stores = {}, {}, []

        def open_group(m, c):
            lo, hi = CHUNKS[c]
            bank = free_banks[0]
            free_banks.remove(bank)
            whole_bank = psum.tile([P, BANK_COLS], F32, name="bank%d" % bank)
            accs[(m, c)] = (bank, whole_bank[:, 0 : hi - lo])

        def multiply(m, c, name, start, stop):
            if name == V:
                codes, plane = b_mx[m * P // B_SPAN]
                lo = m * P % B_SPAN
                lhs, lhs_scale = codes[:, lo : lo + P].bitcast(E4M3), plane[:, lo : lo + P]
            else:
                g = (W0, W1).index(name)
                i, lo = span_of(G_SPANS, m * P)
                lhs, lhs_scale = g_codes[i][:, g, lo : lo + P].bitcast(E5M2), g_planes[i][:, g, lo : lo + P]
            codes, plane = filter_mx[(name, c)]
            nc.tensor.matmul_mx(
                out=accs[(m, c)][1],
                lhsT=lhs,
                lhsT_scale=lhs_scale,
                rhs=codes[:].bitcast(E4M3),
                rhs_scale=plane[:],
                start=start,
                stop=stop,
            )

        def scale_out(m, c):
            lo, hi = CHUNKS[c]
            bank, acc = accs[(m, c)]
            nc.scalar.activation(out=results[m][:, lo:hi], in_=acc, func=COPY, scale=r_cols[:, m : m + 1])
            free_banks.append(bank)

        def add_out(m, c):
            lo, hi = CHUNKS[c]
            bank, acc = accs[(m, c)]
            part = results[m][:, lo:hi]
            nc.vector.scalar_tensor_tensor(
                out=part, in0=acc, scalar=r_cols[:, m : m + 1], in1=part, op0=ALU.mult, op1=ALU.add
            )
            free_banks.append(bank)

        def store(m, lo, hi):
            queue = (nc.sync, nc.scalar)[len(stores) % 2]
            stores.append(m)
            queue.dma_start(out=out[m * P : (m + 1) * P, lo:hi], in_=results[m][:, lo:hi])

        def chunk_done(m, c):
            chunks_done[m] = chunks_done.get(m, 0) + 1
            whole = chunks_done[m] == len(CHUNKS)
            if m == PLAIN_TILES - 1:
                if c == FIRST:
                    store(m, *CHUNKS[FIRST])
                elif whole:
                    store(m, CHUNKS[SECOND][0], J)
            elif whole:
                store(m, 0, J)

        early = [(m, c) for m in range(PLAIN_TILES, TILES) for c in range(len(CHUNKS))]
        plain = [(m, c) for m in range(PLAIN_TILES) for c in range(len(CHUNKS))]

        opening = sorted(early[:BANKS], key=lambda group: (group[1], group[0]))
        for name in (W0, W1):
            grouped = {FIRST: interleave_filter(name, FIRST, nc.vector.tensor_copy)}
            grouped[SECOND] = interleave_filter(name, SECOND, nc.scalar.copy)
            if name == W1:
                load_g_codes(1, nc.scalar, both_passes)
                load_e(1)
            grouped[NARROW] = interleave_filter(name, NARROW, nc.scalar.copy)
            for c in range(len(CHUNKS)):
                quantise_filter(name, c, grouped[c])
            for m, c in opening:
                if name == W0:
                    open_group(m, c)
                multiply(m, c, name, start=name == W0, stop=name == W1)
        for n, (m, c) in enumerate(opening):
            if n == Z1_AFTER:
                load_z(1, nc.scalar)
                load_g_codes(2, nc.sync, both_passes)
                load_g_scales(2)
            scale_out(m, c)
        for m, c in early[BANKS:]:
            open_group(m, c)
            multiply(m, c, W0, start=True, stop=False)
            multiply(m, c, W1, start=False, stop=True)
            scale_out(m, c)
        load_z(2, nc.scalar)
        load_e(2)

        for m, c in plain[:BANKS]:
            open_group(m, c)
            multiply(m, c, W0, start=True, stop=False)
            multiply(m, c, W1, start=False, stop=False)
        make_b((0, 1))
        v_order = (FIRST, NARROW, SECOND)
        grouped = {}
        for n, c in enumerate(v_order):
            grouped[c] = interleave_filter(V, c, nc.vector.tensor_copy)
            if n > 0:
                quantise_filter(V, v_order[n - 1], grouped[v_order[n - 1]])
        quantise_filter(V, v_order[-1], grouped[v_order[-1]])
        for m, c in sorted(plain[:BANKS], key=lambda group: (v_order.index(group[1]), group[0])):
            multiply(m, c, V, start=False, stop=True)
            scale_out(m, c)
            chunk_done(m, c)

        make_b((2, 3))
        partner_step = EARLY_TILES * P // B_SPAN
        for piece in range((PLAIN_TILES - EARLY_TILES) * P // B_SPAN, PLAIN_TILES * P // B_SPAN):
            make_b((piece + partner_step, piece))

        for m, c in plain[BANKS:]:
            partner = m + EARLY_TILES
            if c == FIRST and partner >= PLAIN_TILES:
                for partner_c in range(len(CHUNKS)):
                    open_group(partner, partner_c)
                    multiply(partner, partner_c, V, start=True, stop=True)
                    add_out(partner, partner_c)
                    chunk_done(partner, partner_c)
            open_group(m, c)
            multiply(m, c, W0, start=True, stop=False)
            multiply(m, c, W1, start=False, stop=False)
            multiply(m, c, V, start=False, stop=True)
            scale_out(m, c)
            chunk_done(m, c)
